import numpy as np
import ml_dtypes


def mxq(x, axis, fmt="e4m3"):
    dtype, down = {"e4m3": (ml_dtypes.float8_e4m3fn, 7), "e5m2": (ml_dtypes.float8_e5m2, 14)}[fmt]
    v = np.moveaxis(np.asarray(x, np.float32).astype(ml_dtypes.bfloat16).astype(np.float64), axis, -1)
    blocks = v.reshape(v.shape[:-1] + (-1, 32))
    amax = np.abs(blocks).max(-1, keepdims=True)
    byte = np.maximum(np.where(amax > 0, np.frexp(amax)[1] - 1 + 127, 0) - down, 1)
    scale = np.exp2(byte - 127.0)
    codes = (blocks / scale).astype(np.float32).astype(dtype).astype(np.float64)
    return np.moveaxis((codes * scale).reshape(v.shape), -1, axis)


WIDE = False


def mx_kscale(k):
    if not WIDE:
        return np.ones(k)
    levels = np.array([10, -10, 5, -5, 0])
    if k % 512:
        return np.exp2(np.random.permutation(np.resize(levels, k // 32))).repeat(32)
    a = np.empty((k // 512, 16))
    for p in range(k // 512):
        a[p, :8] = np.random.permutation(np.resize(levels, 8))
        for g in range(8):
            far = levels[np.abs(levels - a[p, g]) >= 10]
            a[p, g + 8] = far[np.random.randint(len(far))]
    return np.exp2(a.ravel()).repeat(32)


def f64(x):
    return np.asarray(x).astype(np.float64)


def striped(idx):
    return np.tile(idx.reshape(-1, 16).T, (8, 1)).astype(np.uint16)


def unstriped(offs):
    return offs[:16].T.reshape(-1).astype(np.int64)


def striped8(idx):
    return np.concatenate([x.reshape(-1, 16).T for x in idx]).astype(np.uint16)


def runs(offs, k):
    lists = np.stack([offs[16 * r : 16 * r + 16].T.reshape(-1) for r in range(8)]).astype(np.int64)
    return lists[np.arange(k) % 512 // 64]


def pack_weight(w):
    k, n = w.shape
    w = f64(np.asarray(w, np.float32).astype(ml_dtypes.bfloat16)).reshape(k // 32, 32, n)
    amax = np.abs(w).max(1)
    byte = np.clip(np.where(amax > 0, np.frexp(amax)[1] - 1 + 127 - 7, 1), 1, 254)
    scaled = (w * np.exp2(127.0 - byte)[:, None, :]).reshape(k, n).astype(np.float32)
    words = np.ascontiguousarray(scaled.reshape(k // 512, 128, 4, n).transpose(0, 1, 3, 2)).astype(ml_dtypes.float8_e4m3fn).view(np.uint8)
    return words, np.ascontiguousarray(byte.astype(np.uint8).reshape(k // 512, 16, n))


def unpack_weight(words, scales):
    g, p, n, _ = words.shape
    vals = np.ascontiguousarray(words).view(ml_dtypes.float8_e4m3fn).astype(np.float64) * np.repeat(np.exp2(scales.astype(np.float64) - 127.0), 8, axis=1)[..., None]
    return vals.transpose(0, 1, 3, 2).reshape(g * 512, n)


def sigmoid(v):
    return 1.0 / (1.0 + np.exp(-np.maximum(v, -700.0)))


K, T, S, H, G = 512, 2048, 512, 512, 2048


def setup_inputs():
    n = np.random.standard_normal
    s = mx_kscale(K)[:, None]
    packed_xT = pack_weight(n((K, T)) * s)
    packed_dT = pack_weight(n((K, G)) / s)
    return {
        "x_words": packed_xT[0],
        "x_scales": packed_xT[1],
        "w1": (n((K, H)) / np.sqrt(K) / s).astype(np.float32),
        "w2": (n((K, H)) / np.sqrt(K) / s).astype(np.float32),
        "gs": (np.random.uniform(0.5, 1.5, (K, 1)) * s).astype(np.float32),
        "d_words": packed_dT[0],
        "d_scales": packed_dT[1],
        "offs": striped(np.random.permutation(T)[:S]),
        "two": striped(np.random.permutation(T)[:S]),
        "la": striped8(np.stack([np.random.permutation(S) for _ in range(8)])),
        "lb": striped8(np.stack([np.random.permutation(S) for _ in range(8)])),
        "kq": striped8(np.random.randint(0, G, (8, H))),
    }


def reference(x_words, x_scales, w1, w2, gs, d_words, d_scales, offs, two, la, lb, kq):
    d_kq = unpack_weight(d_words, d_scales)[np.arange(K)[:, None], runs(kq, K)]
    xq = unpack_weight(x_words, x_scales)[:, unstriped(offs)]
    y = sigmoid(mxq(f64(w1), 0, "e4m3").T @ xq)
    a = y[np.arange(H)[:, None], runs(la, H)]
    x_two = unpack_weight(x_words, x_scales)[:, unstriped(two)]
    c = sigmoid(mxq(f64(w2), 0, "e4m3").T @ x_two)
    b = c[np.arange(H)[:, None], runs(lb, H)]
    m1 = a * b
    z = f64(gs) * (m1 / (m1 + 0.25 * (a - m1) + 0.75 * (b - m1)))
    return 0.0625 * ((d_kq.T @ mxq(z, 0, "e4m3")))

@@ -1,0 +1,181 @@
+import math
+from contextlib import ExitStack
+
+import concourse.mybir as mybir
+
+K, T, S, H, G = 512, 2048, 512, 512, 2048
+FLOPS = 3 * 2 * 512 * 512 * 512
+
+F32 = mybir.dt.float32
+BF16 = mybir.dt.bfloat16
+I32 = mybir.dt.int32
+U32 = mybir.dt.uint32
+U16 = mybir.dt.uint16
+U8 = mybir.dt.uint8
+FP8X4 = mybir.dt.float8_e4m3fn_x4
+ACT = mybir.ActivationFunctionType
+ALU = mybir.AluOpType
+
+P = 128
+PACK = 4
+HALF = 256
+CHUNK = 128
+LAG = 3
+ON_SCALAR = 1
+LN_U = math.log(0.75)
+LN_V = math.log(0.25)
+TINY = 2.0 ** -126
+
+
+def tile_picked_tversky2_none_p_kernel(tc, x_words, x_scales, w1, w2, gs, d_words, d_scales, offs, two, la, lb, kq, out):
+    nc = tc.nc
+    with ExitStack() as ctx:
+        keep = ctx.enter_context(tc.tile_pool(name="keep", bufs=1))
+        psum = ctx.enter_context(tc.psum_pool(name="psum", bufs=1))
+
+        def load_list(src, name):
+            t = keep.tile([P, S // 16], U16, name=name)
+            nc.sync.dma_start(t[:], src)
+            return t
+
+        def load_words(src, name):
+            t = keep.tile([P, T], U32, name=name, align_bytes=64)
+            nc.sync.dma_start(t[:].bitcast(I32), src[0].rearrange("p n t -> p (n t)").bitcast(I32))
+            return t
+
+        def load_weight(src, name):
+            t = keep.tile([P, PACK, H], F32, name=name, align_bytes=64)
+            nc.sync.dma_start(t[:], src.rearrange("(p j) c -> p j c", j=PACK))
+            return t
+
+        xs_tab = keep.tile([P, T], U8, name="xs_tab", align_bytes=64)
+        ds_tab = keep.tile([P, G], U8, name="ds_tab", align_bytes=64)
+        d_plane = keep.tile([P, H], U8, name="d_plane", align_bytes=64)
+        nc.vector.memset(xs_tab[:].bitcast(I32), 0)
+        nc.gpsimd.memset(ds_tab[:].bitcast(I32), 0)
+        nc.gpsimd.memset(d_plane[:].bitcast(I32), 0)
+
+        for r in range(4):
+            nc.sync.dma_start(xs_tab[r:P:32, :].bitcast(I32), x_scales[0, r:16:4, :].bitcast(I32))
+        offs_t = load_list(offs, "offs_t")
+        two_t = load_list(two, "two_t")
+        kq_t = load_list(kq, "kq_t")
+        xw_tab = load_words(x_words, "xw_tab")
+        w1_raw = load_weight(w1, "w1_raw")
+        for r in range(2):
+            nc.sync.dma_start(ds_tab[r:P:16, :].bitcast(I32), d_scales[0, r:16:2, :].bitcast(I32))
+        w2_raw = load_weight(w2, "w2_raw")
+        gs_t = keep.tile([P, PACK], F32, name="gs_t")
+        nc.sync.dma_start(gs_t[:], gs.rearrange("(p t) o -> p (t o)", t=PACK))
+        la_t = load_list(la, "la_t")
+        lb_t = load_list(lb, "lb_t")
+        dw_tab = load_words(d_words, "dw_tab")
+
+        def gather(table, lst, dtype, name):
+            t = keep.tile([P, S], dtype, name=name, align_bytes=64)
+            nc.vector.tensor_copy(t[:], table[:].indirect(lst[:]))
+            return t
+
+        def cast_weight(raw, name, on_vector):
+            g = keep.tile([P, H * PACK], BF16, name=name, align_bytes=64)
+            dst = g[:].rearrange("p (t m j) -> p m t j", t=PACK, j=PACK)
+            src = raw[:].rearrange("p j (m t) -> p m t j", t=PACK)
+            cut = P - on_vector
+            if cut > 0:
+                nc.scalar.copy(dst[:, 0:cut], src[:, 0:cut])
+            if cut < P:
+                nc.vector.tensor_copy(dst[:, cut:P], src[:, cut:P])
+            return g
+
+        def quantize(grouped, width, name):
+            codes = keep.tile([P, width], U32, name=name + "_codes", align_bytes=64)
+            scales = keep.tile([P, width], U8, name=name + "_scales", align_bytes=64)
+            nc.vector.quantize_mx(out=codes[:].bitcast(FP8X4), scales=scales[:], in_=grouped)
+            return codes, scales
+
+        def logits(wq, xw, xs, bank, t):
+            acc = psum.tile([P, S], F32, name="acc%d" % bank, tag="bank%d" % bank)
+            cols = slice(t * P, (t + 1) * P)
+            nc.tensor.matmul_mx(out=acc[:], lhsT=wq[0][:, cols].bitcast(FP8X4), lhsT_scale=wq[1][:, cols],
+                                rhs=xw[:].bitcast(FP8X4), rhs_scale=xs[:], start=True, stop=True)
+            return acc
+
+        x1s = gather(xs_tab, offs_t, U8, "x1s")
+        x2s = gather(xs_tab, two_t, U8, "x2s")
+        x1w = gather(xw_tab, offs_t, U32, "x1w")
+        x2w = gather(xw_tab, two_t, U32, "x2w")
+        w1g = cast_weight(w1_raw, "w1g", 32)
+        w1q = quantize(w1g[:], H, "w1q")
+        dsg = gather(ds_tab, kq_t, U8, "dsg")
+        for r in range(4):
+            nc.sync.dma_start(d_plane[r:P:32, :].bitcast(I32), dsg[16 * (r // 2) + r % 2:P:32, :].bitcast(I32))
+
+        u_win = []
+        for t in range(PACK):
+            acc = logits(w1q, x1w, x1s, t, t)
+            e = keep.tile([P, S], F32, name="u_win%d" % t, align_bytes=64)
+            func = ACT.Copy if t >= PACK - ON_SCALAR else ACT.Exp
+            nc.scalar.activation(e[:], acc[:], func, scale=-1.0, bias=LN_U)
+            u_win.append(e)
+            if t == 0:
+                w2g = cast_weight(w2_raw, "w2g", 96)
+                w2q = quantize(w2g[:], H, "w2q")
+        v_win = []
+        for t in range(PACK):
+            acc = logits(w2q, x2w, x2s, PACK + t, t)
+            e = keep.tile([P, S], F32, name="v_win%d" % t, align_bytes=64)
+            nc.scalar.activation(e[:], acc[:], ACT.Exp, scale=-1.0, bias=LN_V)
+            v_win.append(e)
+
+        part = []
+        for t in range(PACK):
+            a = keep.tile([P, S], F32, name="part%d" % t, align_bytes=64)
+            for h in range(S // HALF):
+                picked = u_win[t][:].indirect(la_t[:, h * HALF // 16:(h + 1) * HALF // 16])
+                if t >= PACK - ON_SCALAR:
+                    nc.scalar.activation(a[:, h * HALF:(h + 1) * HALF], picked, ACT.Exp)
+                else:
+                    nc.vector.tensor_copy(a[:, h * HALF:(h + 1) * HALF], picked)
+            part.append(a)
+        dw = gather(dw_tab, kq_t, U32, "dw")
+
+        gs_sign = keep.tile([P, PACK], BF16, name="gs_sign", align_bytes=64)
+        nc.scalar.activation(gs_sign[:], gs_t[:], ACT.Sign)
+        gs_abs = keep.tile([P, PACK], F32, name="gs_abs")
+        nc.scalar.activation(gs_abs[:], gs_t[:], ACT.Abs)
+        gs_floor = keep.tile([P, PACK], F32, name="gs_floor")
+        nc.vector.tensor_scalar_max(gs_floor[:], gs_abs[:], TINY)
+        gs_inv = keep.tile([P, PACK], F32, name="gs_inv")
+        nc.vector.reciprocal(gs_inv[:], gs_floor[:])
+
+        out_rows = out.rearrange("(m p) j -> p m j", p=P)
+        n = CHUNK
+        for c in range(S // n):
+            j0 = c * n
+            den = keep.tile([P, PACK, n], F32, name="den%d" % c, tag="lag%d" % (c - LAG) if c >= LAG else "den%d" % c, align_bytes=64)
+            for t in range(PACK):
+                nc.vector.tensor_tensor(den[:, t, :], v_win[t][:].indirect(lb_t[:, j0 // 16:(j0 + n) // 16]),
+                                        part[t][:, j0:j0 + n], ALU.add)
+            root = keep.tile([P, PACK, n], F32, name="root%d" % c, align_bytes=64)
+            for t in range(PACK):
+                nc.scalar.activation(root[:, t, :], den[:, t, :], ACT.Abs_reciprocal_sqrt,
+                                     scale=gs_inv[:, t:t + 1], bias=gs_inv[:, t:t + 1])
+            inv = keep.tile([P, n, PACK], BF16, name="inv%d" % c, tag="lag%d" % c, align_bytes=64)
+            nc.scalar.activation(inv[:].rearrange("p (c i) t -> p c t i", i=4),
+                                 root[:].rearrange("p t (c i) -> p c t i", i=4), ACT.Square)
+            zb = keep.tile([P, n, PACK], BF16, name="zb%d" % c, align_bytes=64)
+            nc.vector.tensor_tensor(zb[:], inv[:], gs_sign[:].unsqueeze(1).to_broadcast([P, n, PACK]), ALU.mult)
+            zq = quantize(zb[:].rearrange("p j t -> p (j t)"), n, "z%d" % c)
+            for half in range(2):
+                bank = 2 * c + half
+                acc = psum.tile([P, 2, n], F32, name="o_acc%d" % bank, tag="bank%d" % bank)
+                for m in range(2):
+                    cols = slice((2 * half + m) * P, (2 * half + m + 1) * P)
+                    nc.tensor.matmul_mx(out=acc[:, m, :], lhsT=dw[:, cols].bitcast(FP8X4), lhsT_scale=d_plane[:, cols],
+                                        rhs=zq[0][:].bitcast(FP8X4), rhs_scale=zq[1][:], start=True, stop=True)
+                res = keep.tile([P, 2, n], F32, name="res%d" % bank, align_bytes=64)
+                if c == S // n - 1 and half == 1:
+                    nc.vector.tensor_scalar_mul(res[:], acc[:], 0.0625)
+                else:
+                    nc.scalar.activation(res[:], acc[:], ACT.Copy, scale=0.0625)
+                nc.sync.dma_start(out_rows[:, 2 * half:2 * half + 2, j0:j0 + n], res[:])

@@ -18,10 +18,9 @@ ALU = mybir.AluOpType
 
 P = 128
 PACK = 4
-HALF = 256
-CHUNK = 128
-LAG = 3
-ON_SCALAR = 1
+CHUNKS = (128, 256, 128)
+LAST = PACK - 1
+ORDER = (LAST, 0, 1, 2)
 LN_U = math.log(0.75)
 LN_V = math.log(0.25)
 TINY = 2.0 ** -126
@@ -52,21 +51,24 @@ def tile_picked_tversky2_none_p_kernel(tc, x_words, x_scales, w1, w2, gs, d_word
         ds_tab = keep.tile([P, G], U8, name="ds_tab", align_bytes=64)
         d_plane = keep.tile([P, H], U8, name="d_plane", align_bytes=64)
         nc.vector.memset(xs_tab[:].bitcast(I32), 0)
-        nc.gpsimd.memset(ds_tab[:].bitcast(I32), 0)
-        nc.gpsimd.memset(d_plane[:].bitcast(I32), 0)
+        nc.vector.memset(ds_tab[:].bitcast(I32), 0)
+        nc.vector.memset(d_plane[:].bitcast(I32), 0)
+        u_win = [keep.tile([P, 2 * S if t < LAST else S], F32, name="u_win%d" % t, align_bytes=64) for t in range(PACK)]
+        for t in range(LAST):
+            nc.vector.memset(u_win[t][:, S:], 0.0)
 
         for r in range(4):
             nc.sync.dma_start(xs_tab[r:P:32, :].bitcast(I32), x_scales[0, r:16:4, :].bitcast(I32))
         offs_t = load_list(offs, "offs_t")
         two_t = load_list(two, "two_t")
         kq_t = load_list(kq, "kq_t")
-        xw_tab = load_words(x_words, "xw_tab")
         w1_raw = load_weight(w1, "w1_raw")
         for r in range(2):
             nc.sync.dma_start(ds_tab[r:P:16, :].bitcast(I32), d_scales[0, r:16:2, :].bitcast(I32))
-        w2_raw = load_weight(w2, "w2_raw")
         gs_t = keep.tile([P, PACK], F32, name="gs_t")
         nc.sync.dma_start(gs_t[:], gs.rearrange("(p t) o -> p (t o)", t=PACK))
+        xw_tab = load_words(x_words, "xw_tab")
+        w2_raw = load_weight(w2, "w2_raw")
         la_t = load_list(la, "la_t")
         lb_t = load_list(lb, "lb_t")
         dw_tab = load_words(d_words, "dw_tab")
@@ -81,10 +83,8 @@ def tile_picked_tversky2_none_p_kernel(tc, x_words, x_scales, w1, w2, gs, d_word
             dst = g[:].rearrange("p (t m j) -> p m t j", t=PACK, j=PACK)
             src = raw[:].rearrange("p j (m t) -> p m t j", t=PACK)
             cut = P - on_vector
-            if cut > 0:
-                nc.scalar.copy(dst[:, 0:cut], src[:, 0:cut])
-            if cut < P:
-                nc.vector.tensor_copy(dst[:, cut:P], src[:, cut:P])
+            nc.scalar.copy(dst[:, 0:cut], src[:, 0:cut])
+            nc.vector.tensor_copy(dst[:, cut:P], src[:, cut:P])
             return g
 
         def quantize(grouped, width, name):
@@ -102,21 +102,26 @@ def tile_picked_tversky2_none_p_kernel(tc, x_words, x_scales, w1, w2, gs, d_word
 
         x1s = gather(xs_tab, offs_t, U8, "x1s")
         x2s = gather(xs_tab, two_t, U8, "x2s")
+        w1g = cast_weight(w1_raw, "w1g", 64)
+        w1q = quantize(w1g[:], H, "w1q")
         x1w = gather(xw_tab, offs_t, U32, "x1w")
         x2w = gather(xw_tab, two_t, U32, "x2w")
-        w1g = cast_weight(w1_raw, "w1g", 32)
-        w1q = quantize(w1g[:], H, "w1q")
         dsg = gather(ds_tab, kq_t, U8, "dsg")
         for r in range(4):
             nc.sync.dma_start(d_plane[r:P:32, :].bitcast(I32), dsg[16 * (r // 2) + r % 2:P:32, :].bitcast(I32))
 
-        u_win = []
+        gs_sign = keep.tile([P, PACK], BF16, name="gs_sign", align_bytes=64)
+        nc.scalar.activation(gs_sign[:], gs_t[:], ACT.Sign)
+        gs_abs = keep.tile([P, PACK], F32, name="gs_abs")
+        nc.scalar.activation(gs_abs[:], gs_t[:], ACT.Abs)
+        gs_floor = keep.tile([P, PACK], F32, name="gs_floor")
+        nc.scalar.activation(gs_floor[:], gs_abs[:], ACT.Copy, bias=TINY)
+        gs_inv = keep.tile([P, PACK], F32, name="gs_inv")
+        nc.vector.reciprocal(gs_inv[:], gs_floor[:])
+
         for t in range(PACK):
             acc = logits(w1q, x1w, x1s, t, t)
-            e = keep.tile([P, S], F32, name="u_win%d" % t, align_bytes=64)
-            func = ACT.Copy if t >= PACK - ON_SCALAR else ACT.Exp
-            nc.scalar.activation(e[:], acc[:], func, scale=-1.0, bias=LN_U)
-            u_win.append(e)
+            nc.scalar.activation(u_win[t][:, 0:S], acc[:], ACT.Exp if t < LAST else ACT.Copy, scale=-1.0, bias=LN_U)
             if t == 0:
                 w2g = cast_weight(w2_raw, "w2g", 96)
                 w2q = quantize(w2g[:], H, "w2q")
@@ -127,55 +132,70 @@ def tile_picked_tversky2_none_p_kernel(tc, x_words, x_scales, w1, w2, gs, d_word
             nc.scalar.activation(e[:], acc[:], ACT.Exp, scale=-1.0, bias=LN_V)
             v_win.append(e)
 
-        part = []
-        for t in range(PACK):
-            a = keep.tile([P, S], F32, name="part%d" % t, align_bytes=64)
-            for h in range(S // HALF):
-                picked = u_win[t][:].indirect(la_t[:, h * HALF // 16:(h + 1) * HALF // 16])
-                if t >= PACK - ON_SCALAR:
-                    nc.scalar.activation(a[:, h * HALF:(h + 1) * HALF], picked, ACT.Exp)
-                else:
-                    nc.vector.tensor_copy(a[:, h * HALF:(h + 1) * HALF], picked)
-            part.append(a)
+        starts = [sum(CHUNKS[:c]) for c in range(len(CHUNKS))]
+        part = [gather(u_win[t], la_t, F32, "part%d" % t) for t in range(LAST)]
+        last_part = []
+        for c, n in enumerate(CHUNKS):
+            a = keep.tile([P, n], F32, name="last_part%d" % c, tag="slot_a" if c == 0 else "last_part%d" % c, align_bytes=64)
+            nc.scalar.activation(a[:], u_win[LAST][:].indirect(la_t[:, starts[c] // 16:(starts[c] + n) // 16]), ACT.Exp)
+            last_part.append(a)
         dw = gather(dw_tab, kq_t, U32, "dw")
 
-        gs_sign = keep.tile([P, PACK], BF16, name="gs_sign", align_bytes=64)
-        nc.scalar.activation(gs_sign[:], gs_t[:], ACT.Sign)
-        gs_abs = keep.tile([P, PACK], F32, name="gs_abs")
-        nc.scalar.activation(gs_abs[:], gs_t[:], ACT.Abs)
-        gs_floor = keep.tile([P, PACK], F32, name="gs_floor")
-        nc.vector.tensor_scalar_max(gs_floor[:], gs_abs[:], TINY)
-        gs_inv = keep.tile([P, PACK], F32, name="gs_inv")
-        nc.vector.reciprocal(gs_inv[:], gs_floor[:])
-
         out_rows = out.rearrange("(m p) j -> p m j", p=P)
-        n = CHUNK
-        for c in range(S // n):
-            j0 = c * n
-            den = keep.tile([P, PACK, n], F32, name="den%d" % c, tag="lag%d" % (c - LAG) if c >= LAG else "den%d" % c, align_bytes=64)
-            for t in range(PACK):
-                nc.vector.tensor_tensor(den[:, t, :], v_win[t][:].indirect(lb_t[:, j0 // 16:(j0 + n) // 16]),
-                                        part[t][:, j0:j0 + n], ALU.add)
-            root = keep.tile([P, PACK, n], F32, name="root%d" % c, align_bytes=64)
-            for t in range(PACK):
+        inv = []
+        accs = []
+
+        def divide(c):
+            n, j0 = CHUNKS[c], starts[c]
+            den = keep.tile([P, PACK, n], F32, name="den%d" % c, tag=("den0", "slot_a", "slot_b")[c], align_bytes=64)
+            for t in ORDER:
+                other = part[t][:, j0:j0 + n] if t < LAST else last_part[c][:]
+                nc.vector.tensor_tensor(den[:, t, :], v_win[t][:].indirect(lb_t[:, j0 // 16:(j0 + n) // 16]), other, ALU.add)
+            root = keep.tile([P, PACK, n], F32, name="root%d" % c, tag="root", align_bytes=64)
+            for t in ORDER:
                 nc.scalar.activation(root[:, t, :], den[:, t, :], ACT.Abs_reciprocal_sqrt,
                                      scale=gs_inv[:, t:t + 1], bias=gs_inv[:, t:t + 1])
-            inv = keep.tile([P, n, PACK], BF16, name="inv%d" % c, tag="lag%d" % c, align_bytes=64)
-            nc.scalar.activation(inv[:].rearrange("p (c i) t -> p c t i", i=4),
+            z_abs = keep.tile([P, n, PACK], BF16, name="z_abs%d" % c, tag="slot_b" if c == 0 else "z_abs%d" % c, align_bytes=64)
+            nc.scalar.activation(z_abs[:].rearrange("p (c i) t -> p c t i", i=4),
                                  root[:].rearrange("p t (c i) -> p c t i", i=4), ACT.Square)
+            inv.append(z_abs)
+
+        def product(c):
+            n = CHUNKS[c]
             zb = keep.tile([P, n, PACK], BF16, name="zb%d" % c, align_bytes=64)
-            nc.vector.tensor_tensor(zb[:], inv[:], gs_sign[:].unsqueeze(1).to_broadcast([P, n, PACK]), ALU.mult)
+            nc.vector.tensor_tensor(zb[:], inv[c][:], gs_sign[:].unsqueeze(1).to_broadcast([P, n, PACK]), ALU.mult)
             zq = quantize(zb[:].rearrange("p j t -> p (j t)"), n, "z%d" % c)
-            for half in range(2):
-                bank = 2 * c + half
-                acc = psum.tile([P, 2, n], F32, name="o_acc%d" % bank, tag="bank%d" % bank)
-                for m in range(2):
-                    cols = slice((2 * half + m) * P, (2 * half + m + 1) * P)
+            per_bank = 1 if c == len(CHUNKS) - 1 else 2
+            banks = []
+            for m0 in range(0, PACK, per_bank):
+                bank = 2 * c + m0 // per_bank
+                acc = psum.tile([P, per_bank, n], F32, name="o_acc%d" % bank, tag="bank%d" % bank)
+                for m in range(per_bank):
+                    cols = slice((m0 + m) * P, (m0 + m + 1) * P)
                     nc.tensor.matmul_mx(out=acc[:, m, :], lhsT=dw[:, cols].bitcast(FP8X4), lhsT_scale=d_plane[:, cols],
                                         rhs=zq[0][:].bitcast(FP8X4), rhs_scale=zq[1][:], start=True, stop=True)
-                res = keep.tile([P, 2, n], F32, name="res%d" % bank, align_bytes=64)
-                if c == S // n - 1 and half == 1:
-                    nc.vector.tensor_scalar_mul(res[:], acc[:], 0.0625)
+                banks.append(acc)
+            accs.append(banks)
+
+        def store(c):
+            n, j0 = CHUNKS[c], starts[c]
+            res = keep.tile([P, PACK, n], F32, name="res%d" % c, tag="slot_b" if c == 0 else "res%d" % c, align_bytes=64)
+            per_bank = PACK // len(accs[c])
+            for b, acc in enumerate(accs[c]):
+                rows = res[:, b * per_bank:(b + 1) * per_bank, :]
+                if per_bank == 1 and b % 2 == 1:
+                    nc.vector.tensor_scalar_mul(rows, acc[:], 0.0625)
                 else:
-                    nc.scalar.activation(res[:], acc[:], ACT.Copy, scale=0.0625)
-                nc.sync.dma_start(out_rows[:, 2 * half:2 * half + 2, j0:j0 + n], res[:])
+                    nc.scalar.activation(rows, acc[:], ACT.Copy, scale=0.0625)
+                if (b + 1) * per_bank % 2 == 0:
+                    m1 = (b + 1) * per_bank
+                    nc.sync.dma_start(out_rows[:, m1 - 2:m1, j0:j0 + n], res[:, m1 - 2:m1, :])
+
+        divide(0)
+        divide(1)
+        product(0)
+        divide(2)
+        product(1)
+        product(2)
+        for c in range(len(CHUNKS)):
+            store(c)

@@ -58,7 +58,8 @@ def tile_picked_tversky2_none_p_kernel(tc, x_words, x_scales, w1, w2, gs, d_word
             nc.vector.memset(u_win[t][:, S:], 0.0)
 
         for r in range(4):
-            nc.sync.dma_start(xs_tab[r:P:32, :].bitcast(I32), x_scales[0, r:16:4, :].bitcast(I32))
+            queue = nc.sync if r < 2 else nc.scalar
+            queue.dma_start(xs_tab[r:P:32, :].bitcast(I32), x_scales[0, r:16:4, :].bitcast(I32))
         offs_t = load_list(offs, "offs_t")
         two_t = load_list(two, "two_t")
         kq_t = load_list(kq, "kq_t")
@@ -79,11 +80,12 @@ def tile_picked_tversky2_none_p_kernel(tc, x_words, x_scales, w1, w2, gs, d_word
             return t
 
         def cast_weight(raw, name, on_vector):
-            g = keep.tile([P, H * PACK], BF16, name=name, align_bytes=64)
+            g = keep.tile([P, H * PACK], BF16, name=name, tag=name, align_bytes=64)
             dst = g[:].rearrange("p (t m j) -> p m t j", t=PACK, j=PACK)
             src = raw[:].rearrange("p j (m t) -> p m t j", t=PACK)
             cut = P - on_vector
-            nc.scalar.copy(dst[:, 0:cut], src[:, 0:cut])
+            if cut > 0:
+                nc.scalar.copy(dst[:, 0:cut], src[:, 0:cut])
             nc.vector.tensor_copy(dst[:, cut:P], src[:, cut:P])
             return g
 
@@ -102,7 +104,7 @@ def tile_picked_tversky2_none_p_kernel(tc, x_words, x_scales, w1, w2, gs, d_word
 
         x1s = gather(xs_tab, offs_t, U8, "x1s")
         x2s = gather(xs_tab, two_t, U8, "x2s")
-        w1g = cast_weight(w1_raw, "w1g", 64)
+        w1g = cast_weight(w1_raw, "w1g", 48)
         w1q = quantize(w1g[:], H, "w1q")
         x1w = gather(xw_tab, offs_t, U32, "x1w")
         x2w = gather(xw_tab, two_t, U32, "x2w")
@@ -119,12 +121,11 @@ def tile_picked_tversky2_none_p_kernel(tc, x_words, x_scales, w1, w2, gs, d_word
         gs_inv = keep.tile([P, PACK], F32, name="gs_inv")
         nc.vector.reciprocal(gs_inv[:], gs_floor[:])
 
+        w2g = cast_weight(w2_raw, "w2g", 128)
+        w2q = quantize(w2g[:], H, "w2q")
         for t in range(PACK):
             acc = logits(w1q, x1w, x1s, t, t)
             nc.scalar.activation(u_win[t][:, 0:S], acc[:], ACT.Exp if t < LAST else ACT.Copy, scale=-1.0, bias=LN_U)
-            if t == 0:
-                w2g = cast_weight(w2_raw, "w2g", 96)
-                w2q = quantize(w2g[:], H, "w2q")
         v_win = []
         for t in range(PACK):
             acc = logits(w2q, x2w, x2s, PACK + t, t)
@@ -133,7 +134,10 @@ def tile_picked_tversky2_none_p_kernel(tc, x_words, x_scales, w1, w2, gs, d_word
             v_win.append(e)
 
         starts = [sum(CHUNKS[:c]) for c in range(len(CHUNKS))]
-        part = [gather(u_win[t], la_t, F32, "part%d" % t) for t in range(LAST)]
+        parts = keep.tile([P, LAST, S], F32, name="parts", tag="w2g", align_bytes=64)
+        part = [parts[:, t, :] for t in range(LAST)]
+        for t in range(LAST):
+            nc.vector.tensor_copy(part[t], u_win[t][:].indirect(la_t[:]))
         last_part = []
         for c, n in enumerate(CHUNKS):
             a = keep.tile([P, n], F32, name="last_part%d" % c, tag="slot_a" if c == 0 else "last_part%d" % c, align_bytes=64)
@@ -179,7 +183,7 @@ def tile_picked_tversky2_none_p_kernel(tc, x_words, x_scales, w1, w2, gs, d_word
 
         def store(c):
             n, j0 = CHUNKS[c], starts[c]
-            res = keep.tile([P, PACK, n], F32, name="res%d" % c, tag="slot_b" if c == 0 else "res%d" % c, align_bytes=64)
+            res = keep.tile([P, PACK, n], F32, name="res%d" % c, tag="slot_a" if c == 0 else "res%d" % c, align_bytes=64)
             per_bank = PACK // len(accs[c])
             for b, acc in enumerate(accs[c]):
                 rows = res[:, b * per_bank:(b + 1) * per_bank, :]

@@ -3,7 +3,7 @@ from contextlib import ExitStack
 
 import concourse.mybir as mybir
 
-K, T, S, H, G = 512, 2048, 512, 512, 2048
+T, S, H, G = 2048, 512, 512, 2048
 FLOPS = 3 * 2 * 512 * 512 * 512
 
 F32 = mybir.dt.float32
@@ -18,12 +18,21 @@ ALU = mybir.AluOpType
 
 P = 128
 PACK = 4
+GROUP = 16
+QUADRANT = 32
+SCALE_ROWS = 16
+BANKS = 8
+LINE = 4
 CHUNKS = (128, 256, 128)
-LAST = PACK - 1
-ORDER = (LAST, 0, 1, 2)
+FIRST_BANK = (0, 2, 6)
+SCALAR_PLANE = PACK - 1
+PLANE_ORDER = (SCALAR_PLANE, 0, 1, 2)
+W1_ON_VECTOR = 48
+WARM_UP_PASSES = 3
 LN_U = math.log(0.75)
 LN_V = math.log(0.25)
 TINY = 2.0 ** -126
+OUT_SCALE = 0.0625
 
 
 def tile_picked_tversky2_none_p_kernel(tc, x_words, x_scales, w1, w2, gs, d_words, d_scales, offs, two, la, lb, kq, out):
@@ -33,39 +42,40 @@ def tile_picked_tversky2_none_p_kernel(tc, x_words, x_scales, w1, w2, gs, d_word
         psum = ctx.enter_context(tc.psum_pool(name="psum", bufs=1))
 
         def load_list(src, name):
-            t = keep.tile([P, S // 16], U16, name=name)
-            nc.sync.dma_start(t[:], src)
-            return t
+            offsets = keep.tile([P, S // GROUP], U16, name=name)
+            nc.sync.dma_start(offsets[:], src)
+            return offsets
 
         def load_words(src, name):
-            t = keep.tile([P, T], U32, name=name, align_bytes=64)
-            nc.sync.dma_start(t[:].bitcast(I32), src[0].rearrange("p n t -> p (n t)").bitcast(I32))
-            return t
+            table = keep.tile([P, T], U32, name=name, align_bytes=64)
+            nc.sync.dma_start(table[:].bitcast(I32), src[0].rearrange("p n t -> p (n t)").bitcast(I32))
+            return table
 
         def load_weight(src, name):
-            t = keep.tile([P, PACK, H], F32, name=name, align_bytes=64)
-            nc.sync.dma_start(t[:], src.rearrange("(p j) c -> p j c", j=PACK))
-            return t
+            raw = keep.tile([P, PACK, H], F32, name=name, tag=name, align_bytes=64)
+            nc.sync.dma_start(raw[:], src.rearrange("(p j) c -> p j c", j=PACK))
+            return raw
 
         xs_tab = keep.tile([P, T], U8, name="xs_tab", align_bytes=64)
         ds_tab = keep.tile([P, G], U8, name="ds_tab", align_bytes=64)
-        d_plane = keep.tile([P, H], U8, name="d_plane", align_bytes=64)
+        d_scale = keep.tile([P, H], U8, name="d_scale", align_bytes=64)
         nc.vector.memset(xs_tab[:].bitcast(I32), 0)
         nc.vector.memset(ds_tab[:].bitcast(I32), 0)
-        nc.vector.memset(d_plane[:].bitcast(I32), 0)
-        u_win = [keep.tile([P, 2 * S if t < LAST else S], F32, name="u_win%d" % t, align_bytes=64) for t in range(PACK)]
-        for t in range(LAST):
+        nc.vector.memset(d_scale[:].bitcast(I32), 0)
+        u_win = [keep.tile([P, S if t == SCALAR_PLANE else 2 * S], F32, name="u_win%d" % t, align_bytes=64)
+                 for t in range(PACK)]
+        for t in range(SCALAR_PLANE):
             nc.vector.memset(u_win[t][:, S:], 0.0)
 
-        for r in range(4):
-            queue = nc.sync if r < 2 else nc.scalar
-            queue.dma_start(xs_tab[r:P:32, :].bitcast(I32), x_scales[0, r:16:4, :].bitcast(I32))
+        for r in range(PACK):
+            queue = nc.sync if r < PACK // 2 else nc.scalar
+            queue.dma_start(xs_tab[r:P:QUADRANT, :].bitcast(I32), x_scales[0, r:SCALE_ROWS:PACK, :].bitcast(I32))
         offs_t = load_list(offs, "offs_t")
         two_t = load_list(two, "two_t")
         kq_t = load_list(kq, "kq_t")
         w1_raw = load_weight(w1, "w1_raw")
         for r in range(2):
-            nc.sync.dma_start(ds_tab[r:P:16, :].bitcast(I32), d_scales[0, r:16:2, :].bitcast(I32))
+            nc.sync.dma_start(ds_tab[r:P:GROUP, :].bitcast(I32), d_scales[0, r:SCALE_ROWS:2, :].bitcast(I32))
         gs_t = keep.tile([P, PACK], F32, name="gs_t")
         nc.sync.dma_start(gs_t[:], gs.rearrange("(p t) o -> p (t o)", t=PACK))
         xw_tab = load_words(x_words, "xw_tab")
@@ -74,20 +84,16 @@ def tile_picked_tversky2_none_p_kernel(tc, x_words, x_scales, w1, w2, gs, d_word
         lb_t = load_list(lb, "lb_t")
         dw_tab = load_words(d_words, "dw_tab")
 
-        def gather(table, lst, dtype, name):
-            t = keep.tile([P, S], dtype, name=name, align_bytes=64)
-            nc.vector.tensor_copy(t[:], table[:].indirect(lst[:]))
-            return t
+        def gather(table, offsets, dtype, name):
+            picked = keep.tile([P, S], dtype, name=name, tag=name, align_bytes=64)
+            nc.vector.tensor_copy(picked[:], table[:].indirect(offsets[:]))
+            return picked
 
-        def cast_weight(raw, name, on_vector):
-            g = keep.tile([P, H * PACK], BF16, name=name, tag=name, align_bytes=64)
-            dst = g[:].rearrange("p (t m j) -> p m t j", t=PACK, j=PACK)
+        def rounding_views(raw, name):
+            grouped = keep.tile([P, H * PACK], BF16, name=name, tag=name, align_bytes=64)
+            dst = grouped[:].rearrange("p (t m j) -> p m t j", t=PACK, j=PACK)
             src = raw[:].rearrange("p j (m t) -> p m t j", t=PACK)
-            cut = P - on_vector
-            if cut > 0:
-                nc.scalar.copy(dst[:, 0:cut], src[:, 0:cut])
-            nc.vector.tensor_copy(dst[:, cut:P], src[:, cut:P])
-            return g
+            return grouped, dst, src
 
         def quantize(grouped, width, name):
             codes = keep.tile([P, width], U32, name=name + "_codes", align_bytes=64)
@@ -95,22 +101,30 @@ def tile_picked_tversky2_none_p_kernel(tc, x_words, x_scales, w1, w2, gs, d_word
             nc.vector.quantize_mx(out=codes[:].bitcast(FP8X4), scales=scales[:], in_=grouped)
             return codes, scales
 
-        def logits(wq, xw, xs, bank, t):
-            acc = psum.tile([P, S], F32, name="acc%d" % bank, tag="bank%d" % bank)
+        def mx_product(acc, lhs_codes, lhs_scales, rhs_codes, rhs_scales):
+            nc.tensor.matmul_mx(out=acc, lhsT=lhs_codes.bitcast(FP8X4), lhsT_scale=lhs_scales,
+                                rhs=rhs_codes.bitcast(FP8X4), rhs_scale=rhs_scales, start=True, stop=True)
+
+        def logits(weight, words, scales, bank, t):
+            acc = psum.tile([P, S], F32, name="logits%d" % bank, tag="bank%d" % bank)
             cols = slice(t * P, (t + 1) * P)
-            nc.tensor.matmul_mx(out=acc[:], lhsT=wq[0][:, cols].bitcast(FP8X4), lhsT_scale=wq[1][:, cols],
-                                rhs=xw[:].bitcast(FP8X4), rhs_scale=xs[:], start=True, stop=True)
+            mx_product(acc[:], weight[0][:, cols], weight[1][:, cols], words[:], scales[:])
             return acc
 
         x1s = gather(xs_tab, offs_t, U8, "x1s")
         x2s = gather(xs_tab, two_t, U8, "x2s")
-        w1g = cast_weight(w1_raw, "w1g", 48)
+        w1g, dst, src = rounding_views(w1_raw, "w1g")
+        cut = P - W1_ON_VECTOR
+        nc.scalar.copy(dst[:, 0:cut], src[:, 0:cut])
+        nc.vector.tensor_copy(dst[:, cut:P], src[:, cut:P])
         w1q = quantize(w1g[:], H, "w1q")
         x1w = gather(xw_tab, offs_t, U32, "x1w")
         x2w = gather(xw_tab, two_t, U32, "x2w")
-        dsg = gather(ds_tab, kq_t, U8, "dsg")
-        for r in range(4):
-            nc.sync.dma_start(d_plane[r:P:32, :].bitcast(I32), dsg[16 * (r // 2) + r % 2:P:32, :].bitcast(I32))
+
+        ds_picked = gather(ds_tab, kq_t, U8, "ds_picked")
+        for r in range(PACK):
+            nc.sync.dma_start(d_scale[r:P:QUADRANT, :].bitcast(I32),
+                              ds_picked[GROUP * (r // 2) + r % 2:P:QUADRANT, :].bitcast(I32))
 
         gs_sign = keep.tile([P, PACK], BF16, name="gs_sign", align_bytes=64)
         nc.scalar.activation(gs_sign[:], gs_t[:], ACT.Sign)
@@ -121,85 +135,111 @@ def tile_picked_tversky2_none_p_kernel(tc, x_words, x_scales, w1, w2, gs, d_word
         gs_inv = keep.tile([P, PACK], F32, name="gs_inv")
         nc.vector.reciprocal(gs_inv[:], gs_floor[:])
 
-        w2g = cast_weight(w2_raw, "w2g", 128)
+        w2g, dst, src = rounding_views(w2_raw, "w2g")
+        nc.vector.tensor_copy(dst, src)
         w2q = quantize(w2g[:], H, "w2q")
+
         for t in range(PACK):
             acc = logits(w1q, x1w, x1s, t, t)
-            nc.scalar.activation(u_win[t][:, 0:S], acc[:], ACT.Exp if t < LAST else ACT.Copy, scale=-1.0, bias=LN_U)
+            nc.scalar.activation(u_win[t][:, 0:S], acc[:], ACT.Copy if t == SCALAR_PLANE else ACT.Exp,
+                                 scale=-1.0, bias=LN_U)
         v_win = []
         for t in range(PACK):
             acc = logits(w2q, x2w, x2s, PACK + t, t)
-            e = keep.tile([P, S], F32, name="v_win%d" % t, align_bytes=64)
-            nc.scalar.activation(e[:], acc[:], ACT.Exp, scale=-1.0, bias=LN_V)
-            v_win.append(e)
+            window = keep.tile([P, S], F32, name="v_win%d" % t, align_bytes=64)
+            nc.scalar.activation(window[:], acc[:], ACT.Exp, scale=-1.0, bias=LN_V)
+            v_win.append(window)
 
         starts = [sum(CHUNKS[:c]) for c in range(len(CHUNKS))]
-        parts = keep.tile([P, LAST, S], F32, name="parts", tag="w2g", align_bytes=64)
-        part = [parts[:, t, :] for t in range(LAST)]
-        for t in range(LAST):
-            nc.vector.tensor_copy(part[t], u_win[t][:].indirect(la_t[:]))
-        last_part = []
+        u_picked = keep.tile([P, SCALAR_PLANE, S], F32, name="u_picked", tag="w2_raw", align_bytes=64)
+        for t in range(SCALAR_PLANE):
+            nc.vector.tensor_copy(u_picked[:, t, :], u_win[t][:].indirect(la_t[:]))
+        u_picked_scalar = []
         for c, n in enumerate(CHUNKS):
-            a = keep.tile([P, n], F32, name="last_part%d" % c, tag="slot_a" if c == 0 else "last_part%d" % c, align_bytes=64)
-            nc.scalar.activation(a[:], u_win[LAST][:].indirect(la_t[:, starts[c] // 16:(starts[c] + n) // 16]), ACT.Exp)
-            last_part.append(a)
+            picked = keep.tile([P, n], F32, name="u_scalar%d" % c, tag="u_scalar%d" % c, align_bytes=64)
+            entries = la_t[:, starts[c] // GROUP:(starts[c] + n) // GROUP]
+            nc.scalar.activation(picked[:], u_win[SCALAR_PLANE][:].indirect(entries), ACT.Exp)
+            u_picked_scalar.append(picked)
         dw = gather(dw_tab, kq_t, U32, "dw")
 
         out_rows = out.rearrange("(m p) j -> p m j", p=P)
-        inv = []
-        accs = []
+        z_abs = []
+        out_accs = []
 
-        def divide(c):
+        def divide(c, sum_tag, root_tag):
             n, j0 = CHUNKS[c], starts[c]
-            den = keep.tile([P, PACK, n], F32, name="den%d" % c, tag=("den0", "slot_a", "slot_b")[c], align_bytes=64)
-            for t in ORDER:
-                other = part[t][:, j0:j0 + n] if t < LAST else last_part[c][:]
-                nc.vector.tensor_tensor(den[:, t, :], v_win[t][:].indirect(lb_t[:, j0 // 16:(j0 + n) // 16]), other, ALU.add)
-            root = keep.tile([P, PACK, n], F32, name="root%d" % c, tag="root", align_bytes=64)
-            for t in ORDER:
-                nc.scalar.activation(root[:, t, :], den[:, t, :], ACT.Abs_reciprocal_sqrt,
+            entries = lb_t[:, j0 // GROUP:(j0 + n) // GROUP]
+            exp_sum = keep.tile([P, PACK, n], F32, name="exp_sum%d" % c, tag=sum_tag, align_bytes=64)
+            for t in PLANE_ORDER:
+                u_term = u_picked_scalar[c][:] if t == SCALAR_PLANE else u_picked[:, t, j0:j0 + n]
+                nc.vector.tensor_tensor(exp_sum[:, t, :], v_win[t][:].indirect(entries), u_term, ALU.add)
+            root = keep.tile([P, PACK, n], F32, name="root%d" % c, tag=root_tag, align_bytes=64)
+            for t in PLANE_ORDER:
+                nc.scalar.activation(root[:, t, :], exp_sum[:, t, :], ACT.Abs_reciprocal_sqrt,
                                      scale=gs_inv[:, t:t + 1], bias=gs_inv[:, t:t + 1])
-            z_abs = keep.tile([P, n, PACK], BF16, name="z_abs%d" % c, tag="slot_b" if c == 0 else "z_abs%d" % c, align_bytes=64)
-            nc.scalar.activation(z_abs[:].rearrange("p (c i) t -> p c t i", i=4),
-                                 root[:].rearrange("p t (c i) -> p c t i", i=4), ACT.Square)
-            inv.append(z_abs)
+            squared = keep.tile([P, n, PACK], BF16, name="z_abs%d" % c, tag="z_abs%d" % c, align_bytes=64)
+            nc.scalar.activation(squared[:].rearrange("p (c i) t -> p c t i", i=LINE),
+                                 root[:].rearrange("p t (c i) -> p c t i", i=LINE), ACT.Square)
+            z_abs.append(squared)
 
-        def product(c):
+        def product(c, blocks_per_bank):
             n = CHUNKS[c]
-            zb = keep.tile([P, n, PACK], BF16, name="zb%d" % c, align_bytes=64)
-            nc.vector.tensor_tensor(zb[:], inv[c][:], gs_sign[:].unsqueeze(1).to_broadcast([P, n, PACK]), ALU.mult)
-            zq = quantize(zb[:].rearrange("p j t -> p (j t)"), n, "z%d" % c)
-            per_bank = 1 if c == len(CHUNKS) - 1 else 2
-            banks = []
-            for m0 in range(0, PACK, per_bank):
-                bank = 2 * c + m0 // per_bank
-                acc = psum.tile([P, per_bank, n], F32, name="o_acc%d" % bank, tag="bank%d" % bank)
-                for m in range(per_bank):
+            z = keep.tile([P, n, PACK], BF16, name="z%d" % c, align_bytes=64)
+            nc.vector.tensor_tensor(z[:], z_abs[c][:], gs_sign[:].unsqueeze(1).to_broadcast([P, n, PACK]), ALU.mult)
+            z_codes, z_scales = quantize(z[:].rearrange("p j t -> p (j t)"), n, "zq%d" % c)
+            accs = []
+            for m0 in range(0, PACK, blocks_per_bank):
+                bank = (FIRST_BANK[c] + m0 // blocks_per_bank) % BANKS
+                acc = psum.tile([P, blocks_per_bank, n], F32, name="out_acc%d_%d" % (c, m0), tag="bank%d" % bank)
+                for m in range(blocks_per_bank):
                     cols = slice((m0 + m) * P, (m0 + m + 1) * P)
-                    nc.tensor.matmul_mx(out=acc[:, m, :], lhsT=dw[:, cols].bitcast(FP8X4), lhsT_scale=d_plane[:, cols],
-                                        rhs=zq[0][:].bitcast(FP8X4), rhs_scale=zq[1][:], start=True, stop=True)
-                banks.append(acc)
-            accs.append(banks)
+                    mx_product(acc[:, m, :], dw[:, cols], d_scale[:, cols], z_codes[:], z_scales[:])
+                accs.append(acc)
+            out_accs.append(accs)
+            return z_codes, z_scales
 
-        def store(c):
-            n, j0 = CHUNKS[c], starts[c]
-            res = keep.tile([P, PACK, n], F32, name="res%d" % c, tag="slot_a" if c == 0 else "res%d" % c, align_bytes=64)
-            per_bank = PACK // len(accs[c])
-            for b, acc in enumerate(accs[c]):
-                rows = res[:, b * per_bank:(b + 1) * per_bank, :]
-                if per_bank == 1 and b % 2 == 1:
-                    nc.vector.tensor_scalar_mul(rows, acc[:], 0.0625)
-                else:
-                    nc.scalar.activation(rows, acc[:], ACT.Copy, scale=0.0625)
-                if (b + 1) * per_bank % 2 == 0:
-                    m1 = (b + 1) * per_bank
-                    nc.sync.dma_start(out_rows[:, m1 - 2:m1, j0:j0 + n], res[:, m1 - 2:m1, :])
+        def warm_up(codes, scales):
+            unused = psum.tile([P, S], F32, name="warm_up", tag="bank%d" % (BANKS - 1))
+            for repeat in range(WARM_UP_PASSES):
+                mx_product(unused[:], codes[:], scales[:], x2w[:], x2s[:])
 
-        divide(0)
-        divide(1)
-        product(0)
-        divide(2)
-        product(1)
-        product(2)
-        for c in range(len(CHUNKS)):
-            store(c)
+        def leave_psum(rows, acc, on_vector):
+            if on_vector:
+                nc.vector.tensor_scalar_mul(rows, acc[:], OUT_SCALE)
+            else:
+                nc.scalar.activation(rows, acc[:], ACT.Copy, scale=OUT_SCALE)
+
+        def store_first():
+            n = CHUNKS[0]
+            res = keep.tile([P, PACK, n], F32, name="res0", tag="u_scalar0", align_bytes=64)
+            for pair in range(2):
+                rows = slice(2 * pair, 2 * pair + 2)
+                leave_psum(res[:, rows, :], out_accs[0][pair], False)
+                nc.sync.dma_start(out_rows[:, rows, 0:n], res[:, rows, :])
+
+        def store_middle():
+            n, j0 = CHUNKS[1], starts[1]
+            for m in range(PACK):
+                on_vector = m == PACK - 1
+                name = "res1_%d" % m
+                res = keep.tile([P, 1, n], F32, name=name, tag="z_abs2" if on_vector else name, align_bytes=64)
+                leave_psum(res[:], out_accs[1][m], on_vector)
+                nc.sync.dma_start(out_rows[:, m:m + 1, j0:j0 + n], res[:])
+
+        def store_last():
+            n, j0 = CHUNKS[2], starts[2]
+            for pair in range(2):
+                res = keep.tile([P, 2, n], F32, name="res2_%d" % pair, align_bytes=64)
+                leave_psum(res[:, 0:1, :], out_accs[2][2 * pair], False)
+                leave_psum(res[:, 1:2, :], out_accs[2][2 * pair + 1], True)
+                nc.sync.dma_start(out_rows[:, 2 * pair:2 * pair + 2, j0:j0 + n], res[:])
+
+        divide(0, "exp_sum0", "root0")
+        divide(1, "u_scalar0", "root1")
+        warm_up(*product(0, 2))
+        divide(2, "root0", "root1")
+        store_first()
+        product(1, 1)
+        product(2, 1)
+        store_middle()
+        store_last()

@@ -28,7 +28,6 @@ FIRST_BANK = (0, 2, 6)
 SCALAR_PLANE = PACK - 1
 PLANE_ORDER = (SCALAR_PLANE, 0, 1, 2)
 W1_ON_VECTOR = 48
-WARM_UP_PASSES = 3
 LN_U = math.log(0.75)
 LN_V = math.log(0.25)
 TINY = 2.0 ** -126
@@ -196,12 +195,6 @@ def tile_picked_tversky2_none_p_kernel(tc, x_words, x_scales, w1, w2, gs, d_word
                     mx_product(acc[:, m, :], dw[:, cols], d_scale[:, cols], z_codes[:], z_scales[:])
                 accs.append(acc)
             out_accs.append(accs)
-            return z_codes, z_scales
-
-        def warm_up(codes, scales):
-            unused = psum.tile([P, S], F32, name="warm_up", tag="bank%d" % (BANKS - 1))
-            for repeat in range(WARM_UP_PASSES):
-                mx_product(unused[:], codes[:], scales[:], x2w[:], x2s[:])
 
         def leave_psum(rows, acc, on_vector):
             if on_vector:
@@ -236,7 +229,7 @@ def tile_picked_tversky2_none_p_kernel(tc, x_words, x_scales, w1, w2, gs, d_word
 
         divide(0, "exp_sum0", "root0")
         divide(1, "u_scalar0", "root1")
-        warm_up(*product(0, 2))
+        product(0, 2)
         divide(2, "root0", "root1")
         store_first()
         product(1, 1)

import math
from contextlib import ExitStack

import concourse.mybir as mybir

T, S, H, G = 2048, 512, 512, 2048
FLOPS = 3 * 2 * 512 * 512 * 512

F32 = mybir.dt.float32
BF16 = mybir.dt.bfloat16
I32 = mybir.dt.int32
U32 = mybir.dt.uint32
U16 = mybir.dt.uint16
U8 = mybir.dt.uint8
FP8X4 = mybir.dt.float8_e4m3fn_x4
ACT = mybir.ActivationFunctionType
ALU = mybir.AluOpType

P = 128
PACK = 4
GROUP = 16
QUADRANT = 32
SCALE_ROWS = 16
BANKS = 8
LINE = 4
CHUNKS = (128, 256, 128)
FIRST_BANK = (0, 2, 6)
SCALAR_PLANE = PACK - 1
PLANE_ORDER = (SCALAR_PLANE, 0, 1, 2)
W1_ON_VECTOR = 48
LN_U = math.log(0.75)
LN_V = math.log(0.25)
TINY = 2.0 ** -126
OUT_SCALE = 0.0625


def tile_picked_tversky2_none_p_kernel(tc, x_words, x_scales, w1, w2, gs, d_words, d_scales, offs, two, la, lb, kq, out):
    nc = tc.nc
    with ExitStack() as ctx:
        keep = ctx.enter_context(tc.tile_pool(name="keep", bufs=1))
        psum = ctx.enter_context(tc.psum_pool(name="psum", bufs=1))

        def load_list(src, name):
            offsets = keep.tile([P, S // GROUP], U16, name=name)
            nc.sync.dma_start(offsets[:], src)
            return offsets

        def load_words(src, name):
            table = keep.tile([P, T], U32, name=name, align_bytes=64)
            nc.sync.dma_start(table[:].bitcast(I32), src[0].rearrange("p n t -> p (n t)").bitcast(I32))
            return table

        def load_weight(src, name):
            raw = keep.tile([P, PACK, H], F32, name=name, tag=name, align_bytes=64)
            nc.sync.dma_start(raw[:], src.rearrange("(p j) c -> p j c", j=PACK))
            return raw

        xs_tab = keep.tile([P, T], U8, name="xs_tab", align_bytes=64)
        ds_tab = keep.tile([P, G], U8, name="ds_tab", align_bytes=64)
        d_scale = keep.tile([P, H], U8, name="d_scale", align_bytes=64)
        nc.vector.memset(xs_tab[:].bitcast(I32), 0)
        nc.vector.memset(ds_tab[:].bitcast(I32), 0)
        nc.vector.memset(d_scale[:].bitcast(I32), 0)
        u_win = [keep.tile([P, S if t == SCALAR_PLANE else 2 * S], F32, name="u_win%d" % t, align_bytes=64)
                 for t in range(PACK)]
        for t in range(SCALAR_PLANE):
            nc.vector.memset(u_win[t][:, S:], 0.0)

        for r in range(PACK):
            queue = nc.sync if r < PACK // 2 else nc.scalar
            queue.dma_start(xs_tab[r:P:QUADRANT, :].bitcast(I32), x_scales[0, r:SCALE_ROWS:PACK, :].bitcast(I32))
        offs_t = load_list(offs, "offs_t")
        two_t = load_list(two, "two_t")
        kq_t = load_list(kq, "kq_t")
        w1_raw = load_weight(w1, "w1_raw")
        for r in range(2):
            nc.sync.dma_start(ds_tab[r:P:GROUP, :].bitcast(I32), d_scales[0, r:SCALE_ROWS:2, :].bitcast(I32))
        gs_t = keep.tile([P, PACK], F32, name="gs_t")
        nc.sync.dma_start(gs_t[:], gs.rearrange("(p t) o -> p (t o)", t=PACK))
        xw_tab = load_words(x_words, "xw_tab")
        w2_raw = load_weight(w2, "w2_raw")
        la_t = load_list(la, "la_t")
        lb_t = load_list(lb, "lb_t")
        dw_tab = load_words(d_words, "dw_tab")

        def gather(table, offsets, dtype, name):
            picked = keep.tile([P, S], dtype, name=name, tag=name, align_bytes=64)
            nc.vector.tensor_copy(picked[:], table[:].indirect(offsets[:]))
            return picked

        def rounding_views(raw, name):
            grouped = keep.tile([P, H * PACK], BF16, name=name, tag=name, align_bytes=64)
            dst = grouped[:].rearrange("p (t m j) -> p m t j", t=PACK, j=PACK)
            src = raw[:].rearrange("p j (m t) -> p m t j", t=PACK)
            return grouped, dst, src

        def quantize(grouped, width, name):
            codes = keep.tile([P, width], U32, name=name + "_codes", align_bytes=64)
            scales = keep.tile([P, width], U8, name=name + "_scales", align_bytes=64)
            nc.vector.quantize_mx(out=codes[:].bitcast(FP8X4), scales=scales[:], in_=grouped)
            return codes, scales

        def mx_product(acc, lhs_codes, lhs_scales, rhs_codes, rhs_scales):
            nc.tensor.matmul_mx(out=acc, lhsT=lhs_codes.bitcast(FP8X4), lhsT_scale=lhs_scales,
                                rhs=rhs_codes.bitcast(FP8X4), rhs_scale=rhs_scales, start=True, stop=True)

        def logits(weight, words, scales, bank, t):
            acc = psum.tile([P, S], F32, name="logits%d" % bank, tag="bank%d" % bank)
            cols = slice(t * P, (t + 1) * P)
            mx_product(acc[:], weight[0][:, cols], weight[1][:, cols], words[:], scales[:])
            return acc

        x1s = gather(xs_tab, offs_t, U8, "x1s")
        x2s = gather(xs_tab, two_t, U8, "x2s")
        w1g, dst, src = rounding_views(w1_raw, "w1g")
        cut = P - W1_ON_VECTOR
        nc.scalar.copy(dst[:, 0:cut], src[:, 0:cut])
        nc.vector.tensor_copy(dst[:, cut:P], src[:, cut:P])
        w1q = quantize(w1g[:], H, "w1q")
        x1w = gather(xw_tab, offs_t, U32, "x1w")
        x2w = gather(xw_tab, two_t, U32, "x2w")

        ds_picked = gather(ds_tab, kq_t, U8, "ds_picked")
        for r in range(PACK):
            nc.sync.dma_start(d_scale[r:P:QUADRANT, :].bitcast(I32),
                              ds_picked[GROUP * (r // 2) + r % 2:P:QUADRANT, :].bitcast(I32))

        gs_sign = keep.tile([P, PACK], BF16, name="gs_sign", align_bytes=64)
        nc.scalar.activation(gs_sign[:], gs_t[:], ACT.Sign)
        gs_abs = keep.tile([P, PACK], F32, name="gs_abs")
        nc.scalar.activation(gs_abs[:], gs_t[:], ACT.Abs)
        gs_floor = keep.tile([P, PACK], F32, name="gs_floor")
        nc.scalar.activation(gs_floor[:], gs_abs[:], ACT.Copy, bias=TINY)
        gs_inv = keep.tile([P, PACK], F32, name="gs_inv")
        nc.vector.reciprocal(gs_inv[:], gs_floor[:])

        w2g, dst, src = rounding_views(w2_raw, "w2g")
        nc.vector.tensor_copy(dst, src)
        w2q = quantize(w2g[:], H, "w2q")

        for t in range(PACK):
            acc = logits(w1q, x1w, x1s, t, t)
            nc.scalar.activation(u_win[t][:, 0:S], acc[:], ACT.Copy if t == SCALAR_PLANE else ACT.Exp,
                                 scale=-1.0, bias=LN_U)
        v_win = []
        for t in range(PACK):
            acc = logits(w2q, x2w, x2s, PACK + t, t)
            window = keep.tile([P, S], F32, name="v_win%d" % t, align_bytes=64)
            nc.scalar.activation(window[:], acc[:], ACT.Exp, scale=-1.0, bias=LN_V)
            v_win.append(window)

        starts = [sum(CHUNKS[:c]) for c in range(len(CHUNKS))]
        u_picked = keep.tile([P, SCALAR_PLANE, S], F32, name="u_picked", tag="w2_raw", align_bytes=64)
        for t in range(SCALAR_PLANE):
            nc.vector.tensor_copy(u_picked[:, t, :], u_win[t][:].indirect(la_t[:]))
        u_picked_scalar = []
        for c, n in enumerate(CHUNKS):
            picked = keep.tile([P, n], F32, name="u_scalar%d" % c, tag="u_scalar%d" % c, align_bytes=64)
            entries = la_t[:, starts[c] // GROUP:(starts[c] + n) // GROUP]
            nc.scalar.activation(picked[:], u_win[SCALAR_PLANE][:].indirect(entries), ACT.Exp)
            u_picked_scalar.append(picked)
        dw = gather(dw_tab, kq_t, U32, "dw")

        out_rows = out.rearrange("(m p) j -> p m j", p=P)
        z_abs = []
        out_accs = []

        def divide(c, sum_tag, root_tag):
            n, j0 = CHUNKS[c], starts[c]
            entries = lb_t[:, j0 // GROUP:(j0 + n) // GROUP]
            exp_sum = keep.tile([P, PACK, n], F32, name="exp_sum%d" % c, tag=sum_tag, align_bytes=64)
            for t in PLANE_ORDER:
                u_term = u_picked_scalar[c][:] if t == SCALAR_PLANE else u_picked[:, t, j0:j0 + n]
                nc.vector.tensor_tensor(exp_sum[:, t, :], v_win[t][:].indirect(entries), u_term, ALU.add)
            root = keep.tile([P, PACK, n], F32, name="root%d" % c, tag=root_tag, align_bytes=64)
            for t in PLANE_ORDER:
                nc.scalar.activation(root[:, t, :], exp_sum[:, t, :], ACT.Abs_reciprocal_sqrt,
                                     scale=gs_inv[:, t:t + 1], bias=gs_inv[:, t:t + 1])
            squared = keep.tile([P, n, PACK], BF16, name="z_abs%d" % c, tag="z_abs%d" % c, align_bytes=64)
            nc.scalar.activation(squared[:].rearrange("p (c i) t -> p c t i", i=LINE),
                                 root[:].rearrange("p t (c i) -> p c t i", i=LINE), ACT.Square)
            z_abs.append(squared)

        def product(c, blocks_per_bank):
            n = CHUNKS[c]
            z = keep.tile([P, n, PACK], BF16, name="z%d" % c, align_bytes=64)
            nc.vector.tensor_tensor(z[:], z_abs[c][:], gs_sign[:].unsqueeze(1).to_broadcast([P, n, PACK]), ALU.mult)
            z_codes, z_scales = quantize(z[:].rearrange("p j t -> p (j t)"), n, "zq%d" % c)
            accs = []
            for m0 in range(0, PACK, blocks_per_bank):
                bank = (FIRST_BANK[c] + m0 // blocks_per_bank) % BANKS
                acc = psum.tile([P, blocks_per_bank, n], F32, name="out_acc%d_%d" % (c, m0), tag="bank%d" % bank)
                for m in range(blocks_per_bank):
                    cols = slice((m0 + m) * P, (m0 + m + 1) * P)
                    mx_product(acc[:, m, :], dw[:, cols], d_scale[:, cols], z_codes[:], z_scales[:])
                accs.append(acc)
            out_accs.append(accs)

        def leave_psum(rows, acc, on_vector):
            if on_vector:
                nc.vector.tensor_scalar_mul(rows, acc[:], OUT_SCALE)
            else:
                nc.scalar.activation(rows, acc[:], ACT.Copy, scale=OUT_SCALE)

        def store_first():
            n = CHUNKS[0]
            res = keep.tile([P, PACK, n], F32, name="res0", tag="u_scalar0", align_bytes=64)
            for pair in range(2):
                rows = slice(2 * pair, 2 * pair + 2)
                leave_psum(res[:, rows, :], out_accs[0][pair], False)
                nc.sync.dma_start(out_rows[:, rows, 0:n], res[:, rows, :])

        def store_middle():
            n, j0 = CHUNKS[1], starts[1]
            for m in range(PACK):
                on_vector = m == PACK - 1
                name = "res1_%d" % m
                res = keep.tile([P, 1, n], F32, name=name, tag="z_abs2" if on_vector else name, align_bytes=64)
                leave_psum(res[:], out_accs[1][m], on_vector)
                nc.sync.dma_start(out_rows[:, m:m + 1, j0:j0 + n], res[:])

        def store_last():
            n, j0 = CHUNKS[2], starts[2]
            for pair in range(2):
                res = keep.tile([P, 2, n], F32, name="res2_%d" % pair, align_bytes=64)
                leave_psum(res[:, 0:1, :], out_accs[2][2 * pair], False)
                leave_psum(res[:, 1:2, :], out_accs[2][2 * pair + 1], True)
                nc.sync.dma_start(out_rows[:, 2 * pair:2 * pair + 2, j0:j0 + n], res[:])

        divide(0, "exp_sum0", "root0")
        divide(1, "u_scalar0", "root1")
        product(0, 2)
        divide(2, "root0", "root1")
        store_first()
        product(1, 1)
        product(2, 1)
        store_middle()
        store_last()
